import numpy as np
import ml_dtypes


def mxq(x, axis, fmt="e4m3"):
    dtype, down = {"e4m3": (ml_dtypes.float8_e4m3fn, 7), "e5m2": (ml_dtypes.float8_e5m2, 14)}[fmt]
    v = np.moveaxis(np.asarray(x, np.float32).astype(ml_dtypes.bfloat16).astype(np.float64), axis, -1)
    blocks = v.reshape(v.shape[:-1] + (-1, 32))
    amax = np.abs(blocks).max(-1, keepdims=True)
    byte = np.maximum(np.where(amax > 0, np.frexp(amax)[1] - 1 + 127, 0) - down, 1)
    scale = np.exp2(byte - 127.0)
    codes = (blocks / scale).astype(np.float32).astype(dtype).astype(np.float64)
    return np.moveaxis((codes * scale).reshape(v.shape), -1, axis)


WIDE = False


def mx_kscale(k):
    if not WIDE:
        return np.ones(k)
    levels = np.array([10, -10, 5, -5, 0])
    if k % 512:
        return np.exp2(np.random.permutation(np.resize(levels, k // 32))).repeat(32)
    a = np.empty((k // 512, 16))
    for p in range(k // 512):
        a[p, :8] = np.random.permutation(np.resize(levels, 8))
        for g in range(8):
            far = levels[np.abs(levels - a[p, g]) >= 10]
            a[p, g + 8] = far[np.random.randint(len(far))]
    return np.exp2(a.ravel()).repeat(32)


def f64(x):
    return np.asarray(x).astype(np.float64)


def striped(idx):
    return np.tile(idx.reshape(-1, 16).T, (8, 1)).astype(np.uint16)


def unstriped(offs):
    return offs[:16].T.reshape(-1).astype(np.int64)


E2M1 = np.array([0.0, 0.5, 1.0, 1.5, 2.0, 3.0, 4.0, 6.0, -0.0, -0.5, -1.0, -1.5, -2.0, -3.0, -4.0, -6.0])


def pack_weight(w, fmt):
    k, n = w.shape
    w = f64(np.asarray(w, np.float32).astype(ml_dtypes.bfloat16)).reshape(k // 32, 32, n)
    amax = np.abs(w).max(1)
    if fmt == "e4m3":
        byte = np.frexp(amax)[1] - 1 + 127 - 7
    else:
        mant, ex = np.frexp(amax / 6.0)
        byte = np.where(mant > 0.5, ex, ex - 1) + 127
    byte = np.clip(np.where(amax > 0, byte, 1), 1, 254)
    scaled = (w * np.exp2(127.0 - byte)[:, None, :]).reshape(k, n).astype(np.float32)
    by_word = np.ascontiguousarray(scaled.reshape(k // 512, 128, 4, n).transpose(0, 1, 3, 2))
    if fmt == "e4m3":
        words = by_word.astype(ml_dtypes.float8_e4m3fn).view(np.uint8)
    else:
        c = by_word.astype(ml_dtypes.float4_e2m1fn).view(np.uint8) & 0xF
        words = (c[..., 0::2] | (c[..., 1::2] << 4)).reshape(k // 512, 128, 2 * n)
    return np.ascontiguousarray(words), np.ascontiguousarray(byte.astype(np.uint8).reshape(k // 512, 16, n))


def unpack_weight(words, scales, fmt):
    g, _, n = scales.shape
    words = np.ascontiguousarray(words).reshape(g, 128, n, -1)
    if fmt == "e4m3":
        vals = words.view(ml_dtypes.float8_e4m3fn).astype(np.float64)
    else:
        nib = np.empty((g, 128, n, 4), np.uint8)
        nib[..., 0::2] = words & 0xF
        nib[..., 1::2] = words >> 4
        vals = E2M1[nib]
    vals = vals * np.repeat(np.exp2(scales.astype(np.float64) - 127.0), 8, axis=1)[..., None]
    return vals.transpose(0, 1, 3, 2).reshape(g * 512, n)


def gelu(v):
    return 0.5 * v * (1.0 + np.tanh(np.sqrt(2.0 / np.pi) * (v + 0.044715 * v**3)))


K, T, S, K2, H, N = 1024, 4096, 1024, 512, 1024, 512

def setup_inputs():
    n = np.random.standard_normal
    s = mx_kscale(K)[:, None]
    s2 = mx_kscale(K2)[:, None]
    u = mx_kscale(H)[:, None]
    d = {}
    d["tab_words"], d["tab_scales"] = pack_weight(n((K, T)) * s, "e4m3")
    d["offs"] = striped(np.random.permutation(T)[:S])
    d["xs_words"], d["xs_scales"] = pack_weight(n((K2, S)) * s2, "e4m3")
    d["w1"] = (n((K, H)) / K**0.5 / s).astype(np.float32)
    d["w2_words"], d["w2_scales"] = pack_weight(n((K2, H)) / K2**0.5 / s2, "e2m1")
    d["gain"] = (np.exp(0.3 * n(H)) * u[:, 0]).astype(np.float32)
    d["w3"] = (n((H, N)) / H**0.5 / u).astype(np.float32)
    return d

def reference(tab_words, tab_scales, offs, xs_words, xs_scales, w1, w2_words, w2_scales, gain, w3):
    v = unpack_weight(tab_words, tab_scales, "e4m3")[:, unstriped(offs)]
    xs = unpack_weight(xs_words, xs_scales, "e4m3")
    w2 = unpack_weight(w2_words, w2_scales, "e2m1")
    a = mxq(f64(w1), 0, "e4m3").T @ v
    b = w2.T @ xs
    z = (np.square(a) - np.square(b)) * f64(gain)[:, None]
    y = mxq(f64(w3), 0, "e4m3").T @ mxq(z, 0, "e4m3")
    out = np.log(1.0 + np.abs(y))
    return out

@@ -1,0 +1,257 @@
+from contextlib import ExitStack
+
+import concourse.mybir as mybir
+
+K, T, S, K2, H, N = 1024, 4096, 1024, 512, 1024, 512
+FLOPS = 2 * S * H * (K + K2 + N)
+
+F32 = mybir.dt.float32
+BF16 = mybir.dt.bfloat16
+I32 = mybir.dt.int32
+U32 = mybir.dt.uint32
+U16 = mybir.dt.uint16
+U8 = mybir.dt.uint8
+FP8X4 = mybir.dt.float8_e4m3fn_x4
+FP4X4 = mybir.dt.float4_e2m1fn_x4
+ALU = mybir.AluOpType
+ACT = mybir.ActivationFunctionType
+
+P = 128
+PACK = 4
+PASS = P * PACK
+BANK = 512
+CHUNK = 256
+LINE = 4
+
+
+def tile_list_olive_adulteration_scores_kernel(
+    tc, tab_words, tab_scales, offs, xs_words, xs_scales, w1, w2_words, w2_scales, gain, w3, out
+):
+    nc = tc.nc
+    k_passes = K // PASS
+    r_passes = H // PASS
+    halves = S // BANK
+
+    with ExitStack() as ctx:
+        keep = ctx.enter_context(tc.tile_pool(name="keep", bufs=1))
+        ring = ctx.enter_context(tc.tile_pool(name="ring", bufs=2))
+        feat_psum = ctx.enter_context(tc.psum_pool(name="feat_psum", bufs=4))
+        score_psum = ctx.enter_context(tc.psum_pool(name="score_psum", bufs=4))
+
+        w2_plane_raw = keep.tile([P, H], U8, align_bytes=64)
+        xs_plane = keep.tile([P, S], U8, align_bytes=64)
+        tab_plane = keep.tile([P, T], U8, align_bytes=64)
+        nc.gpsimd.memset(w2_plane_raw[:].bitcast(I32), 0)
+        nc.gpsimd.memset(xs_plane[:].bitcast(I32), 0)
+        nc.gpsimd.memset(tab_plane[:].bitcast(I32), 0)
+
+        def load_plane(plane, scales):
+            rows = 4 * scales.shape[0]
+            for q in range(4):
+                nc.sync.dma_start(
+                    plane[32 * q : 32 * q + rows, :].bitcast(I32), scales[:, 4 * q : 4 * q + 4, :].bitcast(I32)
+                )
+
+        tab_codes = [keep.tile([P, T], I32, name=f"tab_codes{a}") for a in range(k_passes)]
+
+        def load_table(a, h):
+            cols = slice(h * T // 2, (h + 1) * T // 2)
+            nc.sync.dma_start(tab_codes[a][:, cols], tab_words[a].rearrange("p t i -> p (t i)").bitcast(I32)[:, cols])
+
+        w2_raw = keep.tile([P, 2 * H], U8, align_bytes=64)
+        nc.sync.dma_start(w2_raw[:].bitcast(I32), w2_words[0].bitcast(I32))
+        gain_sb = keep.tile([P, r_passes, PACK], F32)
+        nc.sync.dma_start(gain_sb[:], gain.rearrange("(b p t) -> p b t", p=P, t=PACK))
+        load_plane(w2_plane_raw, w2_scales)
+        xs_codes = keep.tile([P, S], I32, align_bytes=64)
+        nc.sync.dma_start(xs_codes[:], xs_words[0].rearrange("p c i -> p (c i)").bitcast(I32))
+        load_table(0, 0)
+        load_plane(xs_plane, xs_scales)
+        load_table(0, 1)
+        offsets = keep.tile([P, S // 16], U16)
+        nc.sync.dma_start(offsets[:], offs)
+        load_table(1, 0)
+        load_table(1, 1)
+        load_plane(tab_plane, tab_scales)
+        w1_raw = {}
+        for b in range(r_passes):
+            for a in range(k_passes):
+                raw = keep.tile([P, PACK, PASS], F32, name=f"w1_raw{a}{b}")
+                rows = w1[a * PASS : (a + 1) * PASS, b * PASS : (b + 1) * PASS]
+                nc.sync.dma_start(raw[:], rows.rearrange("(p i) c -> p i c", i=PACK))
+                w1_raw[a, b] = raw
+        w3_raw = []
+        for b in range(r_passes):
+            raw = keep.tile([P, PACK, N], F32, name=f"w3_raw{b}")
+            nc.sync.dma_start(raw[:], w3[b * PASS : (b + 1) * PASS, :].rearrange("(p i) c -> p i c", i=PACK))
+            w3_raw.append(raw)
+
+        g = gain_sb[:].rearrange("p b t -> p (b t)")
+        size = keep.tile([P, r_passes * PACK], F32)
+        nc.vector.scalar_tensor_tensor(size[:], g, -1.0, g, ALU.mult, ALU.max)
+        safe = keep.tile([P, r_passes * PACK], F32)
+        nc.vector.tensor_scalar(safe[:], size[:], 1e-30, None, ALU.max)
+        guess = keep.tile([P, r_passes * PACK], F32)
+        nc.scalar.activation(guess[:], safe[:], ACT.Sqrt)
+        warm = keep.tile([P, 1], F32)
+        nc.scalar.activation(warm[:], guess[:, 0:1], ACT.Ln)
+        positive = keep.tile([P, r_passes * PACK], F32)
+        nc.vector.tensor_scalar(positive[:], g, 0.0, 2.0, ALU.is_ge, ALU.mult)
+        sign = keep.tile([P, r_passes * PACK], F32)
+        nc.vector.tensor_scalar(sign[:], positive[:], -1.0, None, ALU.add)
+        inverse = keep.tile([P, r_passes * PACK], F32)
+        nc.vector.reciprocal(inverse[:], guess[:])
+        ratio = keep.tile([P, r_passes * PACK], F32)
+        nc.vector.scalar_tensor_tensor(ratio[:], size[:], 0.5, inverse[:], ALU.mult, ALU.mult)
+        root = keep.tile([P, r_passes * PACK], F32)
+        nc.vector.scalar_tensor_tensor(root[:], guess[:], 0.5, ratio[:], ALU.mult, ALU.add)
+
+        w2_codes, w2_planes = [], []
+        for b in range(r_passes):
+            codes = keep.tile([P, 2 * PASS], U8, name=f"w2_codes{b}", align_bytes=64)
+            nc.vector.tensor_copy(
+                codes[:].rearrange("p (t q e) -> p q t e", t=PACK, e=2),
+                w2_raw[:, 2 * PASS * b : 2 * PASS * (b + 1)].rearrange("p (q t e) -> p q t e", t=PACK, e=2),
+            )
+            plane = keep.tile([P, PASS], U8, name=f"w2_plane{b}", align_bytes=64)
+            nc.vector.tensor_copy(
+                plane[:].rearrange("p (t q) -> p q t", t=PACK),
+                w2_plane_raw[:, PASS * b : PASS * (b + 1)].rearrange("p (q t) -> p q t", t=PACK),
+            )
+            w2_codes.append(codes)
+            w2_planes.append(plane)
+
+        def square(acc, dst, b, t):
+            nc.scalar.activation(dst, acc[:], ACT.Square, scale=root[:, PACK * b + t : PACK * b + t + 1])
+
+        b_sq = {}
+        for b in range(r_passes):
+            for h in range(halves):
+                cols = slice(h * BANK, (h + 1) * BANK)
+                sq = keep.tile([P, PACK, BANK], F32, name=f"b_sq{b}{h}")
+                for t in range(PACK):
+                    acc = feat_psum.tile([P, BANK], F32, name="acc")
+                    nc.tensor.matmul_mx(
+                        acc[:],
+                        lhsT=w2_codes[b][:, 2 * P * t : 2 * P * (t + 1)].bitcast(FP4X4),
+                        lhsT_scale=w2_planes[b][:, P * t : P * (t + 1)],
+                        rhs=xs_codes[:, cols].bitcast(FP8X4),
+                        rhs_scale=xs_plane[:, cols],
+                        start=True,
+                        stop=True,
+                    )
+                    square(acc, sq[:, t, :], b, t)
+                b_sq[b, h] = sq
+
+        picked_plane = keep.tile([P, S], U8, align_bytes=64)
+        nc.vector.tensor_copy(picked_plane[:], tab_plane[:].indirect(offsets[:]))
+        picked_codes = []
+        for a in range(k_passes):
+            codes = keep.tile([P, S], U32, name=f"picked_codes{a}", align_bytes=64)
+            nc.vector.tensor_copy(codes[:], tab_codes[a][:].bitcast(U32).indirect(offsets[:]))
+            picked_codes.append(codes)
+
+        def quantise(grouped, name):
+            width = grouped.shape[1] // PACK
+            codes = keep.tile([P, width], U32, name=name + "_codes", align_bytes=64)
+            plane = keep.tile([P, width], U8, name=name + "_plane", align_bytes=64)
+            nc.vector.quantize_mx(codes[:].bitcast(FP8X4), plane[:], grouped[:])
+            return codes, plane
+
+        w1_q = {}
+
+        def make_w1(a, b):
+            grouped = ring.tile([P, PACK * PASS], BF16, name="w_grouped", align_bytes=64)
+            nc.vector.tensor_copy(
+                grouped[:].rearrange("p (t q i) -> p q i t", t=PACK, i=PACK),
+                w1_raw[a, b][:].rearrange("p i (q t) -> p q i t", t=PACK),
+            )
+            w1_q[a, b] = quantise(grouped, f"w1q{a}{b}")
+
+        w3_q = {}
+
+        def make_w3(b):
+            grouped = ring.tile([P, PACK * N], BF16, name="w_grouped", align_bytes=64)
+            signs = sign[:, PACK * b : PACK * (b + 1)].unsqueeze(1).unsqueeze(3)
+            nc.vector.tensor_tensor(
+                grouped[:].rearrange("p (c u i) -> p c i u", u=LINE, i=PACK),
+                w3_raw[b][:].rearrange("p i (c u) -> p c i u", u=LINE),
+                signs.broadcast_to([P, N // LINE, PACK, LINE]),
+                ALU.mult,
+            )
+            w3_q[b] = quantise(grouped, f"w3q{b}")
+
+        a_sq = {}
+
+        def make_a(b, h):
+            cols = slice(h * BANK, (h + 1) * BANK)
+            sq = keep.tile([P, PACK, BANK], F32, name=f"a_sq{b}{h}")
+            for t in range(PACK):
+                acc = feat_psum.tile([P, BANK], F32, name="acc")
+                for a in range(k_passes):
+                    codes, plane = w1_q[a, b]
+                    nc.tensor.matmul_mx(
+                        acc[:],
+                        lhsT=codes[:, P * t : P * (t + 1)].bitcast(FP8X4),
+                        lhsT_scale=plane[:, P * t : P * (t + 1)],
+                        rhs=picked_codes[a][:, cols].bitcast(FP8X4),
+                        rhs_scale=picked_plane[4 * a : P, cols],
+                        start=(a == 0),
+                        stop=(a == k_passes - 1),
+                    )
+                square(acc, sq[:, t, :], b, t)
+            a_sq[b, h] = sq
+
+        z_q = {}
+
+        def make_z(b, c):
+            h, first = divmod(c * CHUNK, BANK)
+            cols = slice(first, first + CHUNK)
+            grouped = ring.tile([P, PACK * CHUNK], BF16, name="z_grouped", align_bytes=64, bufs=3)
+            nc.vector.tensor_tensor(
+                grouped[:].rearrange("p (c u t) -> p c t u", u=LINE, t=PACK),
+                a_sq[b, h][:, :, cols].rearrange("p t (c u) -> p c t u", u=LINE),
+                b_sq[b, h][:, :, cols].rearrange("p t (c u) -> p c t u", u=LINE),
+                ALU.subtract,
+            )
+            z_q[b, c] = quantise(grouped, f"zq{b}{c}")
+
+        def make_scores(c):
+            for pair in range(N // (2 * P)):
+                acc = score_psum.tile([P, 2, CHUNK], F32, name="scores")
+                for m in range(2):
+                    n_cols = slice((2 * pair + m) * P, (2 * pair + m + 1) * P)
+                    for b in range(r_passes):
+                        nc.tensor.matmul_mx(
+                            acc[:, m, :],
+                            lhsT=w3_q[b][0][:, n_cols].bitcast(FP8X4),
+                            lhsT_scale=w3_q[b][1][:, n_cols],
+                            rhs=z_q[b, c][0][:].bitcast(FP8X4),
+                            rhs_scale=z_q[b, c][1][:],
+                            start=(b == 0),
+                            stop=(b == r_passes - 1),
+                        )
+                magnitude = ring.tile([P, 2, CHUNK], F32, name="magnitude")
+                nc.scalar.activation(magnitude[:], acc[:], ACT.Abs)
+                result = ring.tile([P, 2, CHUNK], F32, name="result", bufs=4)
+                nc.scalar.activation(result[:], magnitude[:], ACT.Ln, bias=1.0)
+                rows = out[2 * pair * P : 2 * (pair + 1) * P, c * CHUNK : (c + 1) * CHUNK]
+                nc.sync.dma_start(rows.rearrange("(m p) j -> p m j", p=P), result[:])
+
+        make_w1(0, 0)
+        make_w1(1, 0)
+        make_a(0, 0)
+        make_a(0, 1)
+        make_w1(0, 1)
+        make_w1(1, 1)
+        make_a(1, 0)
+        make_a(1, 1)
+        make_z(0, 0)
+        make_w3(0)
+        make_w3(1)
+        make_z(1, 0)
+        make_scores(0)
+        for c in range(1, S // CHUNK):
+            make_z(0, c)
+            make_z(1, c)
+            make_scores(c)

@@ -20,8 +20,9 @@ P = 128
 PACK = 4
 PASS = P * PACK
 BANK = 512
-CHUNK = 256
+CHUNKS = (128, 128, 256, 128, 128, 128, 128)
 LINE = 4
+HALF = 1024
 
 
 def tile_list_olive_adulteration_scores_kernel(
@@ -35,8 +36,7 @@ def tile_list_olive_adulteration_scores_kernel(
     with ExitStack() as ctx:
         keep = ctx.enter_context(tc.tile_pool(name="keep", bufs=1))
         ring = ctx.enter_context(tc.tile_pool(name="ring", bufs=2))
-        feat_psum = ctx.enter_context(tc.psum_pool(name="feat_psum", bufs=4))
-        score_psum = ctx.enter_context(tc.psum_pool(name="score_psum", bufs=4))
+        psum = ctx.enter_context(tc.psum_pool(name="psum", bufs=8))
 
         w2_plane_raw = keep.tile([P, H], U8, align_bytes=64)
         xs_plane = keep.tile([P, S], U8, align_bytes=64)
@@ -58,6 +58,11 @@ def tile_list_olive_adulteration_scores_kernel(
             cols = slice(h * T // 2, (h + 1) * T // 2)
             nc.sync.dma_start(tab_codes[a][:, cols], tab_words[a].rearrange("p t i -> p (t i)").bitcast(I32)[:, cols])
 
+        w3_raw = [keep.tile([P, PACK, N], F32, name=f"w3_raw{b}") for b in range(r_passes)]
+
+        def load_w3(b):
+            nc.sync.dma_start(w3_raw[b][:], w3[b * PASS : (b + 1) * PASS, :].rearrange("(p i) c -> p i c", i=PACK))
+
         w2_raw = keep.tile([P, 2 * H], U8, align_bytes=64)
         nc.sync.dma_start(w2_raw[:].bitcast(I32), w2_words[0].bitcast(I32))
         gain_sb = keep.tile([P, r_passes, PACK], F32)
@@ -65,26 +70,28 @@ def tile_list_olive_adulteration_scores_kernel(
         load_plane(w2_plane_raw, w2_scales)
         xs_codes = keep.tile([P, S], I32, align_bytes=64)
         nc.sync.dma_start(xs_codes[:], xs_words[0].rearrange("p c i -> p (c i)").bitcast(I32))
-        load_table(0, 0)
+        load_w3(0)
         load_plane(xs_plane, xs_scales)
-        load_table(0, 1)
+        load_table(0, 0)
         offsets = keep.tile([P, S // 16], U16)
         nc.sync.dma_start(offsets[:], offs)
+        load_plane(tab_plane, tab_scales)
+        load_table(0, 1)
+        w1_raw = {}
+
+        def load_w1(a, b):
+            raw = keep.tile([P, PACK, PASS], F32, name=f"w1_raw{a}{b}")
+            rows = w1[a * PASS : (a + 1) * PASS, b * PASS : (b + 1) * PASS]
+            nc.sync.dma_start(raw[:], rows.rearrange("(p i) c -> p i c", i=PACK))
+            w1_raw[a, b] = raw
+
+        load_w1(0, 0)
+        load_w1(1, 0)
         load_table(1, 0)
         load_table(1, 1)
-        load_plane(tab_plane, tab_scales)
-        w1_raw = {}
-        for b in range(r_passes):
-            for a in range(k_passes):
-                raw = keep.tile([P, PACK, PASS], F32, name=f"w1_raw{a}{b}")
-                rows = w1[a * PASS : (a + 1) * PASS, b * PASS : (b + 1) * PASS]
-                nc.sync.dma_start(raw[:], rows.rearrange("(p i) c -> p i c", i=PACK))
-                w1_raw[a, b] = raw
-        w3_raw = []
-        for b in range(r_passes):
-            raw = keep.tile([P, PACK, N], F32, name=f"w3_raw{b}")
-            nc.sync.dma_start(raw[:], w3[b * PASS : (b + 1) * PASS, :].rearrange("(p i) c -> p i c", i=PACK))
-            w3_raw.append(raw)
+        load_w1(0, 1)
+        load_w1(1, 1)
+        load_w3(1)
 
         g = gain_sb[:].rearrange("p b t -> p (b t)")
         size = keep.tile([P, r_passes * PACK], F32)
@@ -130,7 +137,7 @@ def tile_list_olive_adulteration_scores_kernel(
                 cols = slice(h * BANK, (h + 1) * BANK)
                 sq = keep.tile([P, PACK, BANK], F32, name=f"b_sq{b}{h}")
                 for t in range(PACK):
-                    acc = feat_psum.tile([P, BANK], F32, name="acc")
+                    acc = psum.tile([P, BANK], F32, name="acc")
                     nc.tensor.matmul_mx(
                         acc[:],
                         lhsT=w2_codes[b][:, 2 * P * t : 2 * P * (t + 1)].bitcast(FP4X4),
@@ -145,41 +152,67 @@ def tile_list_olive_adulteration_scores_kernel(
 
         picked_plane = keep.tile([P, S], U8, align_bytes=64)
         nc.vector.tensor_copy(picked_plane[:], tab_plane[:].indirect(offsets[:]))
-        picked_codes = []
-        for a in range(k_passes):
-            codes = keep.tile([P, S], U32, name=f"picked_codes{a}", align_bytes=64)
-            nc.vector.tensor_copy(codes[:], tab_codes[a][:].bitcast(U32).indirect(offsets[:]))
-            picked_codes.append(codes)
+        picked_codes = {}
+
+        def gather_codes(a, h):
+            codes = keep.tile([P, BANK], U32, name=f"picked_codes{a}{h}", align_bytes=64)
+            entries = offsets[:, h * BANK // 16 : (h + 1) * BANK // 16]
+            nc.vector.tensor_copy(codes[:], tab_codes[a][:].bitcast(U32).indirect(entries))
+            picked_codes[a, h] = codes
+
+        stage = [keep.tile([P, PACK * PASS], BF16, name=f"stage{u}", align_bytes=64) for u in range(3)]
 
         def quantise(grouped, name):
             width = grouped.shape[1] // PACK
             codes = keep.tile([P, width], U32, name=name + "_codes", align_bytes=64)
             plane = keep.tile([P, width], U8, name=name + "_plane", align_bytes=64)
-            nc.vector.quantize_mx(codes[:].bitcast(FP8X4), plane[:], grouped[:])
+            nc.vector.quantize_mx(codes[:].bitcast(FP8X4), plane[:], grouped)
             return codes, plane
 
         w1_q = {}
 
-        def make_w1(a, b):
-            grouped = ring.tile([P, PACK * PASS], BF16, name="w_grouped", align_bytes=64)
-            nc.vector.tensor_copy(
-                grouped[:].rearrange("p (t q i) -> p q i t", t=PACK, i=PACK),
-                w1_raw[a, b][:].rearrange("p i (q t) -> p q i t", t=PACK),
-            )
-            w1_q[a, b] = quantise(grouped, f"w1q{a}{b}")
+        def make_w1(a, b, on_scalar):
+            grouped = stage[1 - a]
+            for u in range(2):
+                cast = nc.scalar.copy if u in on_scalar else nc.vector.tensor_copy
+                cast(
+                    grouped[:, u * HALF : (u + 1) * HALF].rearrange("p (t q i) -> p q i t", t=2, i=PACK),
+                    w1_raw[a, b][:].rearrange("p i (q t) -> p q i t", t=PACK)[:, :, :, 2 * u : 2 * u + 2],
+                )
+            for u in range(2):
+                w1_q[a, b, u] = quantise(grouped[:, u * HALF : (u + 1) * HALF], f"w1q{a}{b}{u}")
 
         w3_q = {}
 
-        def make_w3(b):
-            grouped = ring.tile([P, PACK * N], BF16, name="w_grouped", align_bytes=64)
+        signed_rows = keep.tile([P, PACK, N // 2], BF16)
+
+        def sign_w3_on_scalar(b):
+            for i in range(PACK):
+                nc.scalar.activation(
+                    signed_rows[:, i, :],
+                    w3_raw[b][:, i, N // 2 :],
+                    ACT.Copy,
+                    scale=sign[:, PACK * b + i : PACK * b + i + 1],
+                )
+
+        def make_w3(b, signed):
+            grouped = stage[b]
             signs = sign[:, PACK * b : PACK * (b + 1)].unsqueeze(1).unsqueeze(3)
-            nc.vector.tensor_tensor(
-                grouped[:].rearrange("p (c u i) -> p c i u", u=LINE, i=PACK),
-                w3_raw[b][:].rearrange("p i (c u) -> p c i u", u=LINE),
-                signs.broadcast_to([P, N // LINE, PACK, LINE]),
-                ALU.mult,
-            )
-            w3_q[b] = quantise(grouped, f"w3q{b}")
+            for u in range(2):
+                if signed and u == 1:
+                    nc.vector.tensor_copy(
+                        grouped[:, HALF:].rearrange("p (c v i) -> p c i v", v=LINE, i=PACK),
+                        signed_rows[:].rearrange("p i (c v) -> p c i v", v=LINE),
+                    )
+                    continue
+                nc.vector.tensor_tensor(
+                    grouped[:, u * HALF : (u + 1) * HALF].rearrange("p (c v i) -> p c i v", v=LINE, i=PACK),
+                    w3_raw[b][:, :, u * N // 2 : (u + 1) * N // 2].rearrange("p i (c v) -> p c i v", v=LINE),
+                    signs.broadcast_to([P, N // (2 * LINE), PACK, LINE]),
+                    ALU.mult,
+                )
+            for u in range(2):
+                w3_q[b, u] = quantise(grouped[:, u * HALF : (u + 1) * HALF], f"w3q{b}{u}")
 
         a_sq = {}
 
@@ -187,14 +220,15 @@ def tile_list_olive_adulteration_scores_kernel(
             cols = slice(h * BANK, (h + 1) * BANK)
             sq = keep.tile([P, PACK, BANK], F32, name=f"a_sq{b}{h}")
             for t in range(PACK):
-                acc = feat_psum.tile([P, BANK], F32, name="acc")
+                acc = psum.tile([P, BANK], F32, name="acc")
                 for a in range(k_passes):
-                    codes, plane = w1_q[a, b]
+                    codes, plane = w1_q[a, b, t // 2]
+                    r_cols = slice(P * (t % 2), P * (t % 2 + 1))
                     nc.tensor.matmul_mx(
                         acc[:],
-                        lhsT=codes[:, P * t : P * (t + 1)].bitcast(FP8X4),
-                        lhsT_scale=plane[:, P * t : P * (t + 1)],
-                        rhs=picked_codes[a][:, cols].bitcast(FP8X4),
+                        lhsT=codes[:, r_cols].bitcast(FP8X4),
+                        lhsT_scale=plane[:, r_cols],
+                        rhs=picked_codes[a, h][:].bitcast(FP8X4),
                         rhs_scale=picked_plane[4 * a : P, cols],
                         start=(a == 0),
                         stop=(a == k_passes - 1),
@@ -205,11 +239,13 @@ def tile_list_olive_adulteration_scores_kernel(
         z_q = {}
 
         def make_z(b, c):
-            h, first = divmod(c * CHUNK, BANK)
-            cols = slice(first, first + CHUNK)
-            grouped = ring.tile([P, PACK * CHUNK], BF16, name="z_grouped", align_bytes=64, bufs=3)
+            width = CHUNKS[c]
+            h, first = divmod(sum(CHUNKS[:c]), BANK)
+            cols = slice(first, first + width)
+            side = c % 2
+            grouped = stage[2 * b][:, side * HALF : side * HALF + PACK * width]
             nc.vector.tensor_tensor(
-                grouped[:].rearrange("p (c u t) -> p c t u", u=LINE, t=PACK),
+                grouped.rearrange("p (c u t) -> p c t u", u=LINE, t=PACK),
                 a_sq[b, h][:, :, cols].rearrange("p t (c u) -> p c t u", u=LINE),
                 b_sq[b, h][:, :, cols].rearrange("p t (c u) -> p c t u", u=LINE),
                 ALU.subtract,
@@ -217,41 +253,48 @@ def tile_list_olive_adulteration_scores_kernel(
             z_q[b, c] = quantise(grouped, f"zq{b}{c}")
 
         def make_scores(c):
+            width = CHUNKS[c]
+            first = sum(CHUNKS[:c])
             for pair in range(N // (2 * P)):
-                acc = score_psum.tile([P, 2, CHUNK], F32, name="scores")
+                acc = psum.tile([P, 2, width], F32, name="acc")
                 for m in range(2):
-                    n_cols = slice((2 * pair + m) * P, (2 * pair + m + 1) * P)
+                    n_cols = slice(m * P, (m + 1) * P)
                     for b in range(r_passes):
                         nc.tensor.matmul_mx(
                             acc[:, m, :],
-                            lhsT=w3_q[b][0][:, n_cols].bitcast(FP8X4),
-                            lhsT_scale=w3_q[b][1][:, n_cols],
+                            lhsT=w3_q[b, pair][0][:, n_cols].bitcast(FP8X4),
+                            lhsT_scale=w3_q[b, pair][1][:, n_cols],
                             rhs=z_q[b, c][0][:].bitcast(FP8X4),
                             rhs_scale=z_q[b, c][1][:],
                             start=(b == 0),
                             stop=(b == r_passes - 1),
                         )
-                magnitude = ring.tile([P, 2, CHUNK], F32, name="magnitude")
+                magnitude = ring.tile([P, 2, width], F32, name="magnitude", bufs=4)
                 nc.scalar.activation(magnitude[:], acc[:], ACT.Abs)
-                result = ring.tile([P, 2, CHUNK], F32, name="result", bufs=4)
+                result = ring.tile([P, 2, width], F32, name="result", bufs=9)
                 nc.scalar.activation(result[:], magnitude[:], ACT.Ln, bias=1.0)
-                rows = out[2 * pair * P : 2 * (pair + 1) * P, c * CHUNK : (c + 1) * CHUNK]
+                rows = out[2 * pair * P : 2 * (pair + 1) * P, first : first + width]
                 nc.sync.dma_start(rows.rearrange("(m p) j -> p m j", p=P), result[:])
 
-        make_w1(0, 0)
-        make_w1(1, 0)
+        make_w3(0, False)
+        gather_codes(0, 0)
+        gather_codes(0, 1)
+        make_w1(0, 0, ())
+        make_w1(1, 0, ())
+        gather_codes(1, 0)
+        gather_codes(1, 1)
         make_a(0, 0)
         make_a(0, 1)
-        make_w1(0, 1)
-        make_w1(1, 1)
+        make_w1(0, 1, ())
+        make_w1(1, 1, ())
+        sign_w3_on_scalar(1)
         make_a(1, 0)
         make_a(1, 1)
         make_z(0, 0)
-        make_w3(0)
-        make_w3(1)
+        make_w3(1, True)
         make_z(1, 0)
         make_scores(0)
-        for c in range(1, S // CHUNK):
+        for c in range(1, len(CHUNKS)):
             make_z(0, c)
             make_z(1, c)
             make_scores(c)

from contextlib import ExitStack

import concourse.mybir as mybir

K, T, S, K2, H, N = 1024, 4096, 1024, 512, 1024, 512
FLOPS = 2 * S * H * (K + K2 + N)

F32 = mybir.dt.float32
BF16 = mybir.dt.bfloat16
I32 = mybir.dt.int32
U32 = mybir.dt.uint32
U16 = mybir.dt.uint16
U8 = mybir.dt.uint8
FP8X4 = mybir.dt.float8_e4m3fn_x4
FP4X4 = mybir.dt.float4_e2m1fn_x4
ALU = mybir.AluOpType
ACT = mybir.ActivationFunctionType

P = 128
PACK = 4
PASS = P * PACK
BANK = 512
CHUNKS = (128, 128, 256, 128, 128, 128, 128)
LINE = 4
HALF = 1024


def tile_list_olive_adulteration_scores_kernel(
    tc, tab_words, tab_scales, offs, xs_words, xs_scales, w1, w2_words, w2_scales, gain, w3, out
):
    nc = tc.nc
    k_passes = K // PASS
    r_passes = H // PASS
    halves = S // BANK

    with ExitStack() as ctx:
        keep = ctx.enter_context(tc.tile_pool(name="keep", bufs=1))
        ring = ctx.enter_context(tc.tile_pool(name="ring", bufs=2))
        psum = ctx.enter_context(tc.psum_pool(name="psum", bufs=8))

        w2_plane_raw = keep.tile([P, H], U8, align_bytes=64)
        xs_plane = keep.tile([P, S], U8, align_bytes=64)
        tab_plane = keep.tile([P, T], U8, align_bytes=64)
        nc.gpsimd.memset(w2_plane_raw[:].bitcast(I32), 0)
        nc.gpsimd.memset(xs_plane[:].bitcast(I32), 0)
        nc.gpsimd.memset(tab_plane[:].bitcast(I32), 0)

        def load_plane(plane, scales):
            rows = 4 * scales.shape[0]
            for q in range(4):
                nc.sync.dma_start(
                    plane[32 * q : 32 * q + rows, :].bitcast(I32), scales[:, 4 * q : 4 * q + 4, :].bitcast(I32)
                )

        tab_codes = [keep.tile([P, T], I32, name=f"tab_codes{a}") for a in range(k_passes)]

        def load_table(a, h):
            cols = slice(h * T // 2, (h + 1) * T // 2)
            nc.sync.dma_start(tab_codes[a][:, cols], tab_words[a].rearrange("p t i -> p (t i)").bitcast(I32)[:, cols])

        w3_raw = [keep.tile([P, PACK, N], F32, name=f"w3_raw{b}") for b in range(r_passes)]

        def load_w3(b):
            nc.sync.dma_start(w3_raw[b][:], w3[b * PASS : (b + 1) * PASS, :].rearrange("(p i) c -> p i c", i=PACK))

        w2_raw = keep.tile([P, 2 * H], U8, align_bytes=64)
        nc.sync.dma_start(w2_raw[:].bitcast(I32), w2_words[0].bitcast(I32))
        gain_sb = keep.tile([P, r_passes, PACK], F32)
        nc.sync.dma_start(gain_sb[:], gain.rearrange("(b p t) -> p b t", p=P, t=PACK))
        load_plane(w2_plane_raw, w2_scales)
        xs_codes = keep.tile([P, S], I32, align_bytes=64)
        nc.sync.dma_start(xs_codes[:], xs_words[0].rearrange("p c i -> p (c i)").bitcast(I32))
        load_w3(0)
        load_plane(xs_plane, xs_scales)
        load_table(0, 0)
        offsets = keep.tile([P, S // 16], U16)
        nc.sync.dma_start(offsets[:], offs)
        load_plane(tab_plane, tab_scales)
        load_table(0, 1)
        w1_raw = {}

        def load_w1(a, b):
            raw = keep.tile([P, PACK, PASS], F32, name=f"w1_raw{a}{b}")
            rows = w1[a * PASS : (a + 1) * PASS, b * PASS : (b + 1) * PASS]
            nc.sync.dma_start(raw[:], rows.rearrange("(p i) c -> p i c", i=PACK))
            w1_raw[a, b] = raw

        load_w1(0, 0)
        load_w1(1, 0)
        load_table(1, 0)
        load_table(1, 1)
        load_w1(0, 1)
        load_w1(1, 1)
        load_w3(1)

        g = gain_sb[:].rearrange("p b t -> p (b t)")
        size = keep.tile([P, r_passes * PACK], F32)
        nc.vector.scalar_tensor_tensor(size[:], g, -1.0, g, ALU.mult, ALU.max)
        safe = keep.tile([P, r_passes * PACK], F32)
        nc.vector.tensor_scalar(safe[:], size[:], 1e-30, None, ALU.max)
        guess = keep.tile([P, r_passes * PACK], F32)
        nc.scalar.activation(guess[:], safe[:], ACT.Sqrt)
        warm = keep.tile([P, 1], F32)
        nc.scalar.activation(warm[:], guess[:, 0:1], ACT.Ln)
        positive = keep.tile([P, r_passes * PACK], F32)
        nc.vector.tensor_scalar(positive[:], g, 0.0, 2.0, ALU.is_ge, ALU.mult)
        sign = keep.tile([P, r_passes * PACK], F32)
        nc.vector.tensor_scalar(sign[:], positive[:], -1.0, None, ALU.add)
        inverse = keep.tile([P, r_passes * PACK], F32)
        nc.vector.reciprocal(inverse[:], guess[:])
        ratio = keep.tile([P, r_passes * PACK], F32)
        nc.vector.scalar_tensor_tensor(ratio[:], size[:], 0.5, inverse[:], ALU.mult, ALU.mult)
        root = keep.tile([P, r_passes * PACK], F32)
        nc.vector.scalar_tensor_tensor(root[:], guess[:], 0.5, ratio[:], ALU.mult, ALU.add)

        w2_codes, w2_planes = [], []
        for b in range(r_passes):
            codes = keep.tile([P, 2 * PASS], U8, name=f"w2_codes{b}", align_bytes=64)
            nc.vector.tensor_copy(
                codes[:].rearrange("p (t q e) -> p q t e", t=PACK, e=2),
                w2_raw[:, 2 * PASS * b : 2 * PASS * (b + 1)].rearrange("p (q t e) -> p q t e", t=PACK, e=2),
            )
            plane = keep.tile([P, PASS], U8, name=f"w2_plane{b}", align_bytes=64)
            nc.vector.tensor_copy(
                plane[:].rearrange("p (t q) -> p q t", t=PACK),
                w2_plane_raw[:, PASS * b : PASS * (b + 1)].rearrange("p (q t) -> p q t", t=PACK),
            )
            w2_codes.append(codes)
            w2_planes.append(plane)

        def square(acc, dst, b, t):
            nc.scalar.activation(dst, acc[:], ACT.Square, scale=root[:, PACK * b + t : PACK * b + t + 1])

        b_sq = {}
        for b in range(r_passes):
            for h in range(halves):
                cols = slice(h * BANK, (h + 1) * BANK)
                sq = keep.tile([P, PACK, BANK], F32, name=f"b_sq{b}{h}")
                for t in range(PACK):
                    acc = psum.tile([P, BANK], F32, name="acc")
                    nc.tensor.matmul_mx(
                        acc[:],
                        lhsT=w2_codes[b][:, 2 * P * t : 2 * P * (t + 1)].bitcast(FP4X4),
                        lhsT_scale=w2_planes[b][:, P * t : P * (t + 1)],
                        rhs=xs_codes[:, cols].bitcast(FP8X4),
                        rhs_scale=xs_plane[:, cols],
                        start=True,
                        stop=True,
                    )
                    square(acc, sq[:, t, :], b, t)
                b_sq[b, h] = sq

        picked_plane = keep.tile([P, S], U8, align_bytes=64)
        nc.vector.tensor_copy(picked_plane[:], tab_plane[:].indirect(offsets[:]))
        picked_codes = {}

        def gather_codes(a, h):
            codes = keep.tile([P, BANK], U32, name=f"picked_codes{a}{h}", align_bytes=64)
            entries = offsets[:, h * BANK // 16 : (h + 1) * BANK // 16]
            nc.vector.tensor_copy(codes[:], tab_codes[a][:].bitcast(U32).indirect(entries))
            picked_codes[a, h] = codes

        stage = [keep.tile([P, PACK * PASS], BF16, name=f"stage{u}", align_bytes=64) for u in range(3)]

        def quantise(grouped, name):
            width = grouped.shape[1] // PACK
            codes = keep.tile([P, width], U32, name=name + "_codes", align_bytes=64)
            plane = keep.tile([P, width], U8, name=name + "_plane", align_bytes=64)
            nc.vector.quantize_mx(codes[:].bitcast(FP8X4), plane[:], grouped)
            return codes, plane

        w1_q = {}

        def make_w1(a, b, on_scalar):
            grouped = stage[1 - a]
            for u in range(2):
                cast = nc.scalar.copy if u in on_scalar else nc.vector.tensor_copy
                cast(
                    grouped[:, u * HALF : (u + 1) * HALF].rearrange("p (t q i) -> p q i t", t=2, i=PACK),
                    w1_raw[a, b][:].rearrange("p i (q t) -> p q i t", t=PACK)[:, :, :, 2 * u : 2 * u + 2],
                )
            for u in range(2):
                w1_q[a, b, u] = quantise(grouped[:, u * HALF : (u + 1) * HALF], f"w1q{a}{b}{u}")

        w3_q = {}

        signed_rows = keep.tile([P, PACK, N // 2], BF16)

        def sign_w3_on_scalar(b):
            for i in range(PACK):
                nc.scalar.activation(
                    signed_rows[:, i, :],
                    w3_raw[b][:, i, N // 2 :],
                    ACT.Copy,
                    scale=sign[:, PACK * b + i : PACK * b + i + 1],
                )

        def make_w3(b, signed):
            grouped = stage[b]
            signs = sign[:, PACK * b : PACK * (b + 1)].unsqueeze(1).unsqueeze(3)
            for u in range(2):
                if signed and u == 1:
                    nc.vector.tensor_copy(
                        grouped[:, HALF:].rearrange("p (c v i) -> p c i v", v=LINE, i=PACK),
                        signed_rows[:].rearrange("p i (c v) -> p c i v", v=LINE),
                    )
                    continue
                nc.vector.tensor_tensor(
                    grouped[:, u * HALF : (u + 1) * HALF].rearrange("p (c v i) -> p c i v", v=LINE, i=PACK),
                    w3_raw[b][:, :, u * N // 2 : (u + 1) * N // 2].rearrange("p i (c v) -> p c i v", v=LINE),
                    signs.broadcast_to([P, N // (2 * LINE), PACK, LINE]),
                    ALU.mult,
                )
            for u in range(2):
                w3_q[b, u] = quantise(grouped[:, u * HALF : (u + 1) * HALF], f"w3q{b}{u}")

        a_sq = {}

        def make_a(b, h):
            cols = slice(h * BANK, (h + 1) * BANK)
            sq = keep.tile([P, PACK, BANK], F32, name=f"a_sq{b}{h}")
            for t in range(PACK):
                acc = psum.tile([P, BANK], F32, name="acc")
                for a in range(k_passes):
                    codes, plane = w1_q[a, b, t // 2]
                    r_cols = slice(P * (t % 2), P * (t % 2 + 1))
                    nc.tensor.matmul_mx(
                        acc[:],
                        lhsT=codes[:, r_cols].bitcast(FP8X4),
                        lhsT_scale=plane[:, r_cols],
                        rhs=picked_codes[a, h][:].bitcast(FP8X4),
                        rhs_scale=picked_plane[4 * a : P, cols],
                        start=(a == 0),
                        stop=(a == k_passes - 1),
                    )
                square(acc, sq[:, t, :], b, t)
            a_sq[b, h] = sq

        z_q = {}

        def make_z(b, c):
            width = CHUNKS[c]
            h, first = divmod(sum(CHUNKS[:c]), BANK)
            cols = slice(first, first + width)
            side = c % 2
            grouped = stage[2 * b][:, side * HALF : side * HALF + PACK * width]
            nc.vector.tensor_tensor(
                grouped.rearrange("p (c u t) -> p c t u", u=LINE, t=PACK),
                a_sq[b, h][:, :, cols].rearrange("p t (c u) -> p c t u", u=LINE),
                b_sq[b, h][:, :, cols].rearrange("p t (c u) -> p c t u", u=LINE),
                ALU.subtract,
            )
            z_q[b, c] = quantise(grouped, f"zq{b}{c}")

        def make_scores(c):
            width = CHUNKS[c]
            first = sum(CHUNKS[:c])
            for pair in range(N // (2 * P)):
                acc = psum.tile([P, 2, width], F32, name="acc")
                for m in range(2):
                    n_cols = slice(m * P, (m + 1) * P)
                    for b in range(r_passes):
                        nc.tensor.matmul_mx(
                            acc[:, m, :],
                            lhsT=w3_q[b, pair][0][:, n_cols].bitcast(FP8X4),
                            lhsT_scale=w3_q[b, pair][1][:, n_cols],
                            rhs=z_q[b, c][0][:].bitcast(FP8X4),
                            rhs_scale=z_q[b, c][1][:],
                            start=(b == 0),
                            stop=(b == r_passes - 1),
                        )
                magnitude = ring.tile([P, 2, width], F32, name="magnitude", bufs=4)
                nc.scalar.activation(magnitude[:], acc[:], ACT.Abs)
                result = ring.tile([P, 2, width], F32, name="result", bufs=9)
                nc.scalar.activation(result[:], magnitude[:], ACT.Ln, bias=1.0)
                rows = out[2 * pair * P : 2 * (pair + 1) * P, first : first + width]
                nc.sync.dma_start(rows.rearrange("(m p) j -> p m j", p=P), result[:])

        make_w3(0, False)
        gather_codes(0, 0)
        gather_codes(0, 1)
        make_w1(0, 0, ())
        make_w1(1, 0, ())
        gather_codes(1, 0)
        gather_codes(1, 1)
        make_a(0, 0)
        make_a(0, 1)
        make_w1(0, 1, ())
        make_w1(1, 1, ())
        sign_w3_on_scalar(1)
        make_a(1, 0)
        make_a(1, 1)
        make_z(0, 0)
        make_w3(1, True)
        make_z(1, 0)
        make_scores(0)
        for c in range(1, len(CHUNKS)):
            make_z(0, c)
            make_z(1, c)
            make_scores(c)
